import numpy as np
import ml_dtypes


def mxq(x, axis, fmt="e4m3"):
    dtype, down = {"e4m3": (ml_dtypes.float8_e4m3fn, 7), "e5m2": (ml_dtypes.float8_e5m2, 14)}[fmt]
    v = np.moveaxis(np.asarray(x, np.float32).astype(ml_dtypes.bfloat16).astype(np.float64), axis, -1)
    blocks = v.reshape(v.shape[:-1] + (-1, 32))
    amax = np.abs(blocks).max(-1, keepdims=True)
    byte = np.maximum(np.where(amax > 0, np.frexp(amax)[1] - 1 + 127, 0) - down, 1)
    scale = np.exp2(byte - 127.0)
    codes = (blocks / scale).astype(np.float32).astype(dtype).astype(np.float64)
    return np.moveaxis((codes * scale).reshape(v.shape), -1, axis)


WIDE = False


def mx_kscale(k):
    if not WIDE:
        return np.ones(k)
    levels = np.array([10, -10, 5, -5, 0])
    if k % 512:
        return np.exp2(np.random.permutation(np.resize(levels, k // 32))).repeat(32)
    a = np.empty((k // 512, 16))
    for p in range(k // 512):
        a[p, :8] = np.random.permutation(np.resize(levels, 8))
        for g in range(8):
            far = levels[np.abs(levels - a[p, g]) >= 10]
            a[p, g + 8] = far[np.random.randint(len(far))]
    return np.exp2(a.ravel()).repeat(32)


def f64(x):
    return np.asarray(x).astype(np.float64)


def striped(idx):
    return np.tile(idx.reshape(-1, 16).T, (8, 1)).astype(np.uint16)


def unstriped(offs):
    return offs[:16].T.reshape(-1).astype(np.int64)


def striped8(idx):
    return np.concatenate([x.reshape(-1, 16).T for x in idx]).astype(np.uint16)


def runs(offs, k):
    lists = np.stack([offs[16 * r : 16 * r + 16].T.reshape(-1) for r in range(8)]).astype(np.int64)
    return lists[np.arange(k) % 512 // 64]


def pack_weight(w):
    k, n = w.shape
    w = f64(np.asarray(w, np.float32).astype(ml_dtypes.bfloat16)).reshape(k // 32, 32, n)
    amax = np.abs(w).max(1)
    byte = np.clip(np.where(amax > 0, np.frexp(amax)[1] - 1 + 127 - 7, 1), 1, 254)
    scaled = (w * np.exp2(127.0 - byte)[:, None, :]).reshape(k, n).astype(np.float32)
    words = np.ascontiguousarray(scaled.reshape(k // 512, 128, 4, n).transpose(0, 1, 3, 2)).astype(ml_dtypes.float8_e4m3fn).view(np.uint8)
    return words, np.ascontiguousarray(byte.astype(np.uint8).reshape(k // 512, 16, n))


def unpack_weight(words, scales):
    g, p, n, _ = words.shape
    vals = np.ascontiguousarray(words).view(ml_dtypes.float8_e4m3fn).astype(np.float64) * np.repeat(np.exp2(scales.astype(np.float64) - 127.0), 8, axis=1)[..., None]
    return vals.transpose(0, 1, 3, 2).reshape(g * 512, n)


E2M1 = np.array([0.0, 0.5, 1.0, 1.5, 2.0, 3.0, 4.0, 6.0, -0.0, -0.5, -1.0, -1.5, -2.0, -3.0, -4.0, -6.0])


def pack_fp4(w):
    k, n = w.shape
    w = f64(np.asarray(w, np.float32).astype(ml_dtypes.bfloat16)).reshape(k // 32, 32, n)
    amax = np.abs(w).max(1)
    mant, ex = np.frexp(amax / 6.0)
    byte = np.clip(np.where(amax > 0, np.where(mant > 0.5, ex, ex - 1) + 127, 1), 1, 254)
    scaled = (w * np.exp2(127.0 - byte)[:, None, :]).reshape(k, n).astype(np.float32)
    c = np.ascontiguousarray(scaled.reshape(k // 512, 128, 4, n).transpose(0, 1, 3, 2)).astype(ml_dtypes.float4_e2m1fn).view(np.uint8) & 0xF
    words = (c[..., 0::2] | (c[..., 1::2] << 4)).reshape(k // 512, 128, 2 * n)
    return np.ascontiguousarray(words), np.ascontiguousarray(byte.astype(np.uint8).reshape(k // 512, 16, n))


def unpack_fp4(words, scales):
    g, _, n = scales.shape
    words = np.ascontiguousarray(words).reshape(g, 128, n, 2)
    nib = np.empty((g, 128, n, 4), np.uint8)
    nib[..., 0::2] = words & 0xF
    nib[..., 1::2] = words >> 4
    vals = E2M1[nib] * np.repeat(np.exp2(scales.astype(np.float64) - 127.0), 8, axis=1)[..., None]
    return vals.transpose(0, 1, 3, 2).reshape(g * 512, n)


def sigmoid(v):
    return 1.0 / (1.0 + np.exp(-np.maximum(v, -700.0)))

def planes(y):
    n, m = y.shape
    v = y.astype(np.float32).astype(ml_dtypes.bfloat16).astype(np.float64).reshape(n // 32, 32, m)
    top = np.abs(v).max(1)
    byte = np.clip(np.where(top > 0, np.frexp(top)[1] - 1 + 127 - 7, 1), 1, 254)
    codes = (v * np.exp2(127.0 - byte)[:, None, :]).reshape(n, m).astype(np.float32).astype(ml_dtypes.float8_e4m3fn).view(np.uint8)
    words = codes.reshape(n // 512, 128, 4, m).transpose(0, 1, 3, 2)
    return np.ascontiguousarray(words), np.ascontiguousarray(byte.astype(np.uint8).reshape(n // 512, 16, m))


K, T, S, N, H, G, U = 512, 1024, 512, 512, 512, 2048, 1024


def setup_inputs():
    n = np.random.standard_normal
    s = mx_kscale(K)[:, None]
    u = mx_kscale(S)
    packed_xT = pack_weight(n((K, T)) * s)
    packed_w1 = pack_fp4(n((K, H)) / np.sqrt(K) / s)
    packed_dT = pack_weight(n((K, G)) / s)
    packed_w2 = pack_fp4(n((H, N)) / np.sqrt(H) / u[:, None])
    return {
        "x_words": packed_xT[0],
        "x_scales": packed_xT[1],
        "w1_words": packed_w1[0],
        "w1_scales": packed_w1[1],
        "gs": (np.random.uniform(0.5, 1.5, (K, 1)) * s).astype(np.float32),
        "d_words": packed_dT[0],
        "d_scales": packed_dT[1],
        "mem": n((H, U)).astype(np.float32),
        "res": (1.5 * n((N, U))).astype(np.float32),
        "gn": (np.random.uniform(0.5, 1.5, (H, 1)) * u[:, None]).astype(np.float32),
        "w2_words": packed_w2[0],
        "w2_scales": packed_w2[1],
        "offs": striped(np.random.permutation(T)[:S]),
        "n1": striped8(np.stack([np.random.permutation(S) for _ in range(8)])),
        "n2": striped8(np.stack([np.random.permutation(S) for _ in range(8)])),
        "kidx": striped8(np.random.randint(0, G, (8, H))),
        "n3": striped8(np.stack([np.random.permutation(U)[:S] for _ in range(8)])),
    }


def reference(x_words, x_scales, w1_words, w1_scales, gs, d_words, d_scales, mem, res, gn, w2_words, w2_scales, offs, n1, n2, kidx, n3):
    old = f64(mem)[np.arange(H)[:, None], runs(n3, H)]
    d_kidx = unpack_weight(d_words, d_scales)[np.arange(K)[:, None], runs(kidx, K)]
    xq = unpack_weight(x_words, x_scales)[:, unstriped(offs)]
    y = unpack_fp4(w1_words, w1_scales).T @ xq
    z = f64(gs) * (y + (sigmoid(y[np.arange(H)[:, None], runs(n1, H)])) * (y[np.arange(H)[:, None], runs(n2, H)] - y))
    s = 0.0625 * ((d_kidx.T @ mxq(z, 0, "e4m3")))
    nw = old + sigmoid(s) * (s - old)
    pg = f64(mem).copy()
    pg[np.arange(H)[:, None], runs(n3, H)] = nw
    z2 = f64(gn) * pg
    out_0 = f64(res) + (unpack_fp4(w2_words, w2_scales).T @ mxq(z2, 0, "e4m3"))
    return (out_0,) + planes(out_0)

@@ -1,0 +1,237 @@
+from contextlib import ExitStack
+
+import concourse.mybir as mybir
+
+FLOPS = 1073741824
+
+F32 = mybir.dt.float32
+BF16 = mybir.dt.bfloat16
+I32 = mybir.dt.int32
+U32 = mybir.dt.uint32
+U16 = mybir.dt.uint16
+U8 = mybir.dt.uint8
+FP8X4 = mybir.dt.float8_e4m3fn_x4
+FP4X4 = mybir.dt.float4_e2m1fn_x4
+ACT = mybir.ActivationFunctionType
+ALU = mybir.AluOpType
+
+P = 128
+PACK = 4
+S = 512
+T = 1024
+G = 2048
+U = 1024
+HALF = 256
+CHUNK = 256
+
+
+def load_scale_rows(nc, plane, scales):
+    for q in range(4):
+        nc.sync.dma_start(out=plane[32 * q : 32 * q + 4, :].bitcast(I32), in_=scales[0, 4 * q : 4 * q + 4, :].bitcast(I32))
+
+
+def deal(nc, out, in_, width):
+    nc.vector.tensor_copy(
+        out=out.rearrange("p (t m b) -> p t m b", t=PACK, b=width),
+        in_=in_.rearrange("p (m t b) -> p t m b", t=PACK, b=width),
+    )
+
+
+def woven(ap):
+    return ap.rearrange("p (c i t) -> p c t i", i=4, t=PACK)
+
+
+def by_rows(ap):
+    return ap.rearrange("p t (c i) -> p c t i", i=4)
+
+
+def tile_picked_pqktrackpaget_none_po_kernel(
+    tc, x_words, x_scales, w1_words, w1_scales, gs, d_words, d_scales, mem, res, gn, w2_words, w2_scales,
+    offs, n1, n2, kidx, n3, out_0, out_1, out_2,
+):
+    nc = tc.nc
+    with ExitStack() as ctx:
+        sb = ctx.enter_context(tc.tile_pool(name="sb", bufs=1))
+        ps = ctx.enter_context(tc.psum_pool(name="ps", bufs=1))
+
+        def tile(name, shape, dtype):
+            return sb.tile(shape, dtype, name=name, align_bytes=64)
+
+        def bank(n, shape):
+            return ps.tile(shape, F32, name="bank%d" % n, tag="bank%d" % n)
+
+        def load_list(name, src):
+            t = sb.tile([P, S // 16], U16, name=name)
+            nc.sync.dma_start(t[:], src)
+            return t
+
+        x_sc = tile("x_sc", [P, T], U8)
+        w1_sc = tile("w1_sc", [P, S], U8)
+        w2_sc = tile("w2_sc", [P, S], U8)
+        d_sc = tile("d_sc", [P, G], U8)
+        key_sc = tile("key_sc", [P, S], U8)
+        nc.vector.memset(x_sc[:].bitcast(I32), 0)
+        nc.gpsimd.memset(w1_sc[:].bitcast(I32), 0)
+        nc.vector.memset(d_sc[:].bitcast(I32), 0)
+        nc.gpsimd.memset(w2_sc[:].bitcast(I32), 0)
+        nc.gpsimd.memset(key_sc[:].bitcast(I32), 0)
+        warm = tile("warm", [P, 2], F32)
+        nc.gpsimd.memset(warm[:, 0:1], 0.0)
+        nc.scalar.activation(warm[:, 1:2], warm[:, 0:1], ACT.Sigmoid)
+
+        w1_w = tile("w1_w", [P, 2 * S], U8)
+        nc.sync.dma_start(out=w1_w[:].bitcast(I32), in_=w1_words[0].bitcast(I32))
+        load_scale_rows(nc, x_sc, x_scales)
+        offs_t = load_list("offs_t", offs)
+        x_w = tile("x_w", [P, T], I32)
+        nc.sync.dma_start(out=x_w[:], in_=x_words[0].rearrange("p c r -> p (c r)").bitcast(I32))
+        load_scale_rows(nc, w1_sc, w1_scales)
+        kidx_t = load_list("kidx_t", kidx)
+        nc.sync.dma_start(out=d_sc[0:P:8, :].bitcast(I32), in_=d_scales[0].bitcast(I32))
+        d_w = tile("d_w", [P, G], I32)
+        nc.sync.dma_start(out=d_w[:], in_=d_words[0].rearrange("p c r -> p (c r)").bitcast(I32))
+        n1_t = load_list("n1_t", n1)
+        n2_t = load_list("n2_t", n2)
+        gs_t = tile("gs_t", [P, PACK], F32)
+        nc.sync.dma_start(out=gs_t[:], in_=gs.rearrange("(p t) o -> p (t o)", t=PACK))
+
+        w1_wd = tile("w1_wd", [P, 2 * S], U8)
+        w1_sd = tile("w1_sd", [P, S], U8)
+        xg_sc = tile("xg_sc", [P, S], U8)
+        xg_w = tile("xg_w", [P, S], U32)
+        deal(nc, w1_wd[:], w1_w[:], 2)
+        nc.vector.tensor_copy(xg_sc[:], x_sc[:].indirect(offs_t[:]))
+        nc.vector.tensor_copy(xg_w[:], x_w[:].bitcast(U32).indirect(offs_t[:]))
+        deal(nc, w1_sd[:], w1_sc[:], 1)
+        y_ps = [bank(t, [P, S]) for t in range(PACK)]
+        for t in range(PACK):
+            nc.tensor.matmul_mx(
+                out=y_ps[t][:], lhsT=w1_wd[:, 256 * t : 256 * (t + 1)].bitcast(FP4X4), lhsT_scale=w1_sd[:, P * t : P * (t + 1)],
+                rhs=xg_w[:].bitcast(FP8X4), rhs_scale=xg_sc[:], start=True, stop=True,
+            )
+
+        dg_sc = tile("dg_sc", [P, S], U8)
+        dg_sd = sb.tile([P, S], U8, name="dg_sd", tag="late", align_bytes=64)
+        dg_w = tile("dg_w", [P, S], U32)
+        key_w = tile("key_w", [P, S], U32)
+        nc.vector.tensor_copy(dg_sc[:], d_sc[:].indirect(kidx_t[:]))
+        nc.vector.tensor_copy(dg_w[:], d_w[:].bitcast(U32).indirect(kidx_t[:]))
+        deal(nc, dg_sd[:], dg_sc[:], 1)
+        deal(nc, key_w[:], dg_w[:], 1)
+
+        w2_w = tile("w2_w", [P, 2 * S], U8)
+        nc.sync.dma_start(out=w2_w[:].bitcast(I32), in_=w2_words[0].bitcast(I32))
+        load_scale_rows(nc, w2_sc, w2_scales)
+        w2_wd = tile("w2_wd", [P, 2 * S], U8)
+        w2_sd = tile("w2_sd", [P, S], U8)
+        n3_t = load_list("n3_t", n3)
+        mem_rows = mem.rearrange("(p t) w -> p t w", t=PACK)
+        page = [sb.tile([P, U], F32, name="page%d" % t) for t in range(PACK)]
+        for t in range(PACK):
+            nc.sync.dma_start(out=page[t][:], in_=mem_rows[:, t, :])
+        for j in range(4):
+            nc.sync.dma_start(out=key_sc[j:P:32, :].bitcast(I32), in_=dg_sd[8 * j : P : 32, :].bitcast(I32))
+        gn_t = tile("gn_t", [P, PACK], F32)
+        nc.sync.dma_start(out=gn_t[:], in_=gn.rearrange("(p t) o -> p (t o)", t=PACK))
+        res_t = sb.tile([P, PACK, U], F32, name="res_t", tag="late", align_bytes=64)
+        nc.sync.dma_start(out=res_t[:], in_=res.rearrange("(p t) w -> p t w", t=PACK))
+
+        halves = range(S // HALF)
+        y = [tile("y%d" % t, [P, S], F32) for t in range(PACK)]
+        ys = [tile("ys%d" % t, [P, S], F32) for t in range(PACK)]
+        gate = [tile("gate%d" % h, [P, PACK, HALF], F32) for h in halves]
+        far = [tile("far%d" % h, [P, PACK, HALF], F32) for h in halves]
+        near = [tile("near%d" % h, [P, PACK, HALF], F32) for h in halves]
+        z_bf = [tile("z_bf%d" % h, [P, PACK * HALF], BF16) for h in halves]
+        z_w = [tile("z_w%d" % h, [P, HALF], U32) for h in halves]
+        z_sc = [tile("z_sc%d" % h, [P, HALF], U8) for h in halves]
+        s_ps = [bank(4 + t, [P, S]) for t in range(PACK)]
+        keep = [tile("keep%d" % t, [P, S], F32) for t in range(PACK)]
+        kept = [tile("kept%d" % t, [P, S], F32) for t in range(PACK)]
+        fresh = [tile("fresh%d" % t, [P, S], F32) for t in range(PACK)]
+        lcols = HALF // 16
+        for h in halves:
+            cols = slice(h * HALF, (h + 1) * HALF)
+            lc = slice(h * lcols, (h + 1) * lcols)
+            for t in range(PACK):
+                if h == 0:
+                    nc.scalar.copy(y[t][:], y_ps[t][:])
+                nc.scalar.activation(gate[h][:, t, :], y[t][:].indirect(n1_t[:, lc]), ACT.Sigmoid)
+                if h == 0:
+                    nc.scalar.activation(ys[t][:], y_ps[t][:], ACT.Copy, scale=gs_t[:, t : t + 1])
+                nc.vector.tensor_tensor(far[h][:, t, :], ys[t][:].indirect(n2_t[:, lc]), gate[h][:, t, :], ALU.mult)
+                nc.vector.scalar_tensor_tensor(near[h][:, t, :], gate[h][:, t, :], 1.0, ys[t][:, cols], ALU.subtract, ALU.mult)
+            nc.vector.tensor_tensor(woven(z_bf[h][:]), by_rows(far[h][:]), by_rows(near[h][:]), ALU.subtract)
+            nc.vector.quantize_mx(out=z_w[h][:].bitcast(FP8X4), scales=z_sc[h][:], in_=z_bf[h][:])
+            for t in range(PACK):
+                nc.tensor.matmul_mx(
+                    out=s_ps[t][:, cols], lhsT=key_w[:, P * t : P * (t + 1)].bitcast(FP8X4), lhsT_scale=key_sc[:, P * t : P * (t + 1)],
+                    rhs=z_w[h][:].bitcast(FP8X4), rhs_scale=z_sc[h][:], start=True, stop=True,
+                )
+        for h in halves:
+            cols = slice(h * HALF, (h + 1) * HALF)
+            lc = slice(h * lcols, (h + 1) * lcols)
+            for t in range(PACK):
+                nc.scalar.activation(keep[t][:, cols], s_ps[t][:, cols], ACT.Sigmoid, scale=-0.0625)
+                nc.vector.tensor_tensor(kept[t][:, cols], page[t][:].indirect(n3_t[:, lc]), keep[t][:, cols], ALU.mult)
+        for t in range(PACK):
+            nc.scalar.activation(fresh[t][:], s_ps[t][:], ACT.Silu, scale=0.0625)
+
+        chunks = range(U // CHUNK)
+        z2_bf = [tile("z2_bf%d" % c, [P, CHUNK, PACK], BF16) for c in chunks]
+        for t in range(PACK):
+            nc.vector.tensor_tensor(page[t][:].indirect(n3_t[:]), kept[t][:], fresh[t][:], ALU.add)
+            for c in chunks:
+                nc.scalar.activation(z2_bf[c][:, :, t], page[t][:, c * CHUNK : (c + 1) * CHUNK], ACT.Copy, scale=gn_t[:, t : t + 1])
+
+        deal(nc, w2_wd[:], w2_w[:], 2)
+        deal(nc, w2_sd[:], w2_sc[:], 1)
+
+        out_rows = out_0.rearrange("(p t) w -> p t w", t=PACK)
+        out_words = out_1[0].rearrange("p c r -> p (c r)").bitcast(I32)
+        o_sc = tile("o_sc", [P, U], U8)
+        z2_w = [tile("z2_w%d" % c, [P, CHUNK], U32) for c in chunks]
+        z2_sc = [tile("z2_sc%d" % c, [P, CHUNK], U8) for c in chunks]
+        o = [tile("o%d" % c, [P, PACK, CHUNK], F32) for c in chunks]
+        o_bf = [tile("o_bf%d" % c, [P, PACK * CHUNK], BF16) for c in chunks]
+        o_w = [tile("o_w%d" % c, [P, CHUNK], I32) for c in chunks]
+
+        def project(c):
+            cols = slice(c * CHUNK, (c + 1) * CHUNK)
+            nc.vector.quantize_mx(out=z2_w[c][:].bitcast(FP8X4), scales=z2_sc[c][:], in_=z2_bf[c][:].rearrange("p w t -> p (w t)"))
+            accs = []
+            for pair in range(2):
+                acc = bank(2 * c + pair, [P, 2, CHUNK])
+                accs.append(acc)
+                for e in range(2):
+                    t = 2 * pair + e
+                    nc.tensor.matmul_mx(
+                        out=acc[:, e, :], lhsT=w2_wd[:, 256 * t : 256 * (t + 1)].bitcast(FP4X4), lhsT_scale=w2_sd[:, P * t : P * (t + 1)],
+                        rhs=z2_w[c][:].bitcast(FP8X4), rhs_scale=z2_sc[c][:], start=True, stop=True,
+                    )
+            return accs
+
+        def add_residual(c, accs):
+            cols = slice(c * CHUNK, (c + 1) * CHUNK)
+            for pair in range(2):
+                ts = slice(2 * pair, 2 * pair + 2)
+                nc.vector.tensor_tensor(o[c][:, ts, :], accs[pair][:], res_t[:, ts, cols], ALU.add)
+            nc.sync.dma_start(out=out_rows[:, :, cols], in_=o[c][:])
+            nc.scalar.copy(woven(o_bf[c][:]), by_rows(o[c][:]))
+
+        def hand_on(c):
+            cols = slice(c * CHUNK, (c + 1) * CHUNK)
+            nc.vector.quantize_mx(out=o_w[c][:].bitcast(FP8X4), scales=o_sc[:, cols], in_=o_bf[c][:])
+            nc.sync.dma_start(out=out_words[:, cols], in_=o_w[c][:])
+
+        accs = {}
+        n = len(chunks)
+        for step in range(n + 2):
+            if step < n:
+                accs[step] = project(step)
+            if 1 <= step <= n:
+                add_residual(step - 1, accs[step - 1])
+            if step >= 2:
+                hand_on(step - 2)
+        for q in range(4):
+            nc.sync.dma_start(out=out_2[0, 4 * q : 4 * q + 4, :].bitcast(I32), in_=o_sc[32 * q : 32 * q + 4, :].bitcast(I32))

@@ -22,19 +22,25 @@ T = 1024
 G = 2048
 U = 1024
 HALF = 256
-CHUNK = 256
+CHUNKS = (128, 256, 256, 256, 128)
+SCALED_ON_SCALAR = 1
+ON_VECTOR = 256
 
 
-def load_scale_rows(nc, plane, scales):
+def load_scale_rows(queue, plane, scales):
     for q in range(4):
-        nc.sync.dma_start(out=plane[32 * q : 32 * q + 4, :].bitcast(I32), in_=scales[0, 4 * q : 4 * q + 4, :].bitcast(I32))
+        queue.dma_start(out=plane[32 * q : 32 * q + 4, :].bitcast(I32), in_=scales[0, 4 * q : 4 * q + 4, :].bitcast(I32))
 
 
-def deal(nc, out, in_, width):
-    nc.vector.tensor_copy(
+def deal(engine, out, in_, width):
+    engine.tensor_copy(
         out=out.rearrange("p (t m b) -> p t m b", t=PACK, b=width),
         in_=in_.rearrange("p (m t b) -> p t m b", t=PACK, b=width),
     )
+
+
+def words_of(cols):
+    return slice(PACK * cols.start, PACK * cols.stop)
 
 
 def woven(ap):
@@ -81,28 +87,36 @@ def tile_picked_pqktrackpaget_none_po_kernel(
 
         w1_w = tile("w1_w", [P, 2 * S], U8)
         nc.sync.dma_start(out=w1_w[:].bitcast(I32), in_=w1_words[0].bitcast(I32))
-        load_scale_rows(nc, x_sc, x_scales)
+        load_scale_rows(nc.sync, x_sc, x_scales)
         offs_t = load_list("offs_t", offs)
         x_w = tile("x_w", [P, T], I32)
         nc.sync.dma_start(out=x_w[:], in_=x_words[0].rearrange("p c r -> p (c r)").bitcast(I32))
-        load_scale_rows(nc, w1_sc, w1_scales)
         kidx_t = load_list("kidx_t", kidx)
-        nc.sync.dma_start(out=d_sc[0:P:8, :].bitcast(I32), in_=d_scales[0].bitcast(I32))
+        load_scale_rows(nc.sync, w1_sc, w1_scales)
         d_w = tile("d_w", [P, G], I32)
         nc.sync.dma_start(out=d_w[:], in_=d_words[0].rearrange("p c r -> p (c r)").bitcast(I32))
+        nc.sync.dma_start(out=d_sc[0:P:8, :].bitcast(I32), in_=d_scales[0].bitcast(I32))
         n1_t = load_list("n1_t", n1)
         n2_t = load_list("n2_t", n2)
         gs_t = tile("gs_t", [P, PACK], F32)
-        nc.sync.dma_start(out=gs_t[:], in_=gs.rearrange("(p t) o -> p (t o)", t=PACK))
+        nc.gpsimd.dma_start(out=gs_t[:], in_=gs.rearrange("(p t) o -> p (t o)", t=PACK))
+
+        w2_w = tile("w2_w", [P, 2 * S], U8)
+        nc.gpsimd.dma_start(out=w2_w[:].bitcast(I32), in_=w2_words[0].bitcast(I32))
+        load_scale_rows(nc.gpsimd, w2_sc, w2_scales)
+        w2_wd = tile("w2_wd", [P, 2 * S], U8)
+        w2_sd = tile("w2_sd", [P, S], U8)
+        deal(nc.gpsimd, w2_wd[:], w2_w[:], 2)
+        deal(nc.gpsimd, w2_sd[:], w2_sc[:], 1)
 
         w1_wd = tile("w1_wd", [P, 2 * S], U8)
         w1_sd = tile("w1_sd", [P, S], U8)
         xg_sc = tile("xg_sc", [P, S], U8)
         xg_w = tile("xg_w", [P, S], U32)
-        deal(nc, w1_wd[:], w1_w[:], 2)
+        deal(nc.vector, w1_wd[:], w1_w[:], 2)
         nc.vector.tensor_copy(xg_sc[:], x_sc[:].indirect(offs_t[:]))
         nc.vector.tensor_copy(xg_w[:], x_w[:].bitcast(U32).indirect(offs_t[:]))
-        deal(nc, w1_sd[:], w1_sc[:], 1)
+        deal(nc.vector, w1_sd[:], w1_sc[:], 1)
         y_ps = [bank(t, [P, S]) for t in range(PACK)]
         for t in range(PACK):
             nc.tensor.matmul_mx(
@@ -114,16 +128,11 @@ def tile_picked_pqktrackpaget_none_po_kernel(
         dg_sd = sb.tile([P, S], U8, name="dg_sd", tag="late", align_bytes=64)
         dg_w = tile("dg_w", [P, S], U32)
         key_w = tile("key_w", [P, S], U32)
-        nc.vector.tensor_copy(dg_sc[:], d_sc[:].indirect(kidx_t[:]))
         nc.vector.tensor_copy(dg_w[:], d_w[:].bitcast(U32).indirect(kidx_t[:]))
-        deal(nc, dg_sd[:], dg_sc[:], 1)
-        deal(nc, key_w[:], dg_w[:], 1)
+        nc.vector.tensor_copy(dg_sc[:], d_sc[:].indirect(kidx_t[:]))
+        deal(nc.vector, key_w[:], dg_w[:], 1)
+        deal(nc.vector, dg_sd[:], dg_sc[:], 1)
 
-        w2_w = tile("w2_w", [P, 2 * S], U8)
-        nc.sync.dma_start(out=w2_w[:].bitcast(I32), in_=w2_words[0].bitcast(I32))
-        load_scale_rows(nc, w2_sc, w2_scales)
-        w2_wd = tile("w2_wd", [P, 2 * S], U8)
-        w2_sd = tile("w2_sd", [P, S], U8)
         n3_t = load_list("n3_t", n3)
         mem_rows = mem.rearrange("(p t) w -> p t w", t=PACK)
         page = [sb.tile([P, U], F32, name="page%d" % t) for t in range(PACK)]
@@ -150,61 +159,91 @@ def tile_picked_pqktrackpaget_none_po_kernel(
         kept = [tile("kept%d" % t, [P, S], F32) for t in range(PACK)]
         fresh = [tile("fresh%d" % t, [P, S], F32) for t in range(PACK)]
         lcols = HALF // 16
-        for h in halves:
-            cols = slice(h * HALF, (h + 1) * HALF)
-            lc = slice(h * lcols, (h + 1) * lcols)
-            for t in range(PACK):
-                if h == 0:
-                    nc.scalar.copy(y[t][:], y_ps[t][:])
-                nc.scalar.activation(gate[h][:, t, :], y[t][:].indirect(n1_t[:, lc]), ACT.Sigmoid)
-                if h == 0:
-                    nc.scalar.activation(ys[t][:], y_ps[t][:], ACT.Copy, scale=gs_t[:, t : t + 1])
-                nc.vector.tensor_tensor(far[h][:, t, :], ys[t][:].indirect(n2_t[:, lc]), gate[h][:, t, :], ALU.mult)
-                nc.vector.scalar_tensor_tensor(near[h][:, t, :], gate[h][:, t, :], 1.0, ys[t][:, cols], ALU.subtract, ALU.mult)
+
+        def half(h):
+            return slice(h * HALF, (h + 1) * HALF)
+
+        def list_half(lst, h):
+            return lst[:, h * lcols : (h + 1) * lcols]
+
+        def blend_terms(h, t):
+            nc.scalar.activation(gate[h][:, t, :], y[t][:].indirect(list_half(n1_t, h)), ACT.Sigmoid)
+            nc.vector.scalar_tensor_tensor(near[h][:, t, :], gate[h][:, t, :], 1.0, ys[t][:, half(h)], ALU.subtract, ALU.mult)
+            nc.vector.tensor_tensor(far[h][:, t, :], ys[t][:].indirect(list_half(n2_t, h)), gate[h][:, t, :], ALU.mult)
+
+        def blend(h):
             nc.vector.tensor_tensor(woven(z_bf[h][:]), by_rows(far[h][:]), by_rows(near[h][:]), ALU.subtract)
+
+        def score(h):
             nc.vector.quantize_mx(out=z_w[h][:].bitcast(FP8X4), scales=z_sc[h][:], in_=z_bf[h][:])
             for t in range(PACK):
                 nc.tensor.matmul_mx(
-                    out=s_ps[t][:, cols], lhsT=key_w[:, P * t : P * (t + 1)].bitcast(FP8X4), lhsT_scale=key_sc[:, P * t : P * (t + 1)],
+                    out=s_ps[t][:, half(h)], lhsT=key_w[:, P * t : P * (t + 1)].bitcast(FP8X4), lhsT_scale=key_sc[:, P * t : P * (t + 1)],
                     rhs=z_w[h][:].bitcast(FP8X4), rhs_scale=z_sc[h][:], start=True, stop=True,
                 )
-        for h in halves:
-            cols = slice(h * HALF, (h + 1) * HALF)
-            lc = slice(h * lcols, (h + 1) * lcols)
-            for t in range(PACK):
-                nc.scalar.activation(keep[t][:, cols], s_ps[t][:, cols], ACT.Sigmoid, scale=-0.0625)
-                nc.vector.tensor_tensor(kept[t][:, cols], page[t][:].indirect(n3_t[:, lc]), keep[t][:, cols], ALU.mult)
+                nc.scalar.activation(keep[t][:, half(h)], s_ps[t][:, half(h)], ACT.Sigmoid, scale=-0.0625)
+
+        def weigh_old_half(h, t):
+            nc.vector.tensor_tensor(kept[t][:, half(h)], page[t][:].indirect(list_half(n3_t, h)), keep[t][:, half(h)], ALU.mult)
+
+        for t in range(PACK):
+            nc.scalar.copy(y[t][:], y_ps[t][:])
+            if t < SCALED_ON_SCALAR:
+                nc.scalar.activation(ys[t][:], y_ps[t][:], ACT.Copy, scale=gs_t[:, t : t + 1])
+            else:
+                nc.vector.tensor_scalar(ys[t][:], y[t][:], gs_t[:, t : t + 1], None, ALU.mult)
+            blend_terms(0, t)
+        blend_terms(1, 0)
+        blend(0)
+        blend_terms(1, 1)
+        score(0)
+        blend_terms(1, 2)
+        blend_terms(1, 3)
+        weigh_old_half(0, 0)
+        blend(1)
+        weigh_old_half(0, 1)
+        score(1)
+        weigh_old_half(0, 2)
+        weigh_old_half(0, 3)
+        for t in range(PACK):
+            weigh_old_half(1, t)
         for t in range(PACK):
             nc.scalar.activation(fresh[t][:], s_ps[t][:], ACT.Silu, scale=0.0625)
 
-        chunks = range(U // CHUNK)
-        z2_bf = [tile("z2_bf%d" % c, [P, CHUNK, PACK], BF16) for c in chunks]
+        chunks = range(len(CHUNKS))
+        cols_of = [slice(sum(CHUNKS[:c]), sum(CHUNKS[: c + 1])) for c in chunks]
+        z2_bf = tile("z2_bf", [P, U * PACK], BF16)
+        z2_rows = z2_bf[:].rearrange("p (w t) -> p w t", t=PACK)
         for t in range(PACK):
             nc.vector.tensor_tensor(page[t][:].indirect(n3_t[:]), kept[t][:], fresh[t][:], ALU.add)
-            for c in chunks:
-                nc.scalar.activation(z2_bf[c][:, :, t], page[t][:, c * CHUNK : (c + 1) * CHUNK], ACT.Copy, scale=gn_t[:, t : t + 1])
+            spans = [[slice(0, U)], [slice(0, U)], [slice(ON_VECTOR, U)], [slice(max(cols.start, ON_VECTOR), cols.stop) for cols in cols_of[1:]]][t]
+            for cols in spans:
+                nc.scalar.activation(z2_rows[:, cols, t], page[t][:, cols], ACT.Copy, scale=gn_t[:, t : t + 1])
 
-        deal(nc, w2_wd[:], w2_w[:], 2)
-        deal(nc, w2_sd[:], w2_sc[:], 1)
+        def round_on_vector(cols):
+            for t in (2, 3):
+                nc.vector.tensor_scalar(z2_rows[:, cols, t], page[t][:, cols], gn_t[:, t : t + 1], None, ALU.mult)
+
+        round_on_vector(cols_of[0])
 
         out_rows = out_0.rearrange("(p t) w -> p t w", t=PACK)
         out_words = out_1[0].rearrange("p c r -> p (c r)").bitcast(I32)
         o_sc = tile("o_sc", [P, U], U8)
-        z2_w = [tile("z2_w%d" % c, [P, CHUNK], U32) for c in chunks]
-        z2_sc = [tile("z2_sc%d" % c, [P, CHUNK], U8) for c in chunks]
-        o = [tile("o%d" % c, [P, PACK, CHUNK], F32) for c in chunks]
-        o_bf = [tile("o_bf%d" % c, [P, PACK * CHUNK], BF16) for c in chunks]
-        o_w = [tile("o_w%d" % c, [P, CHUNK], I32) for c in chunks]
+        z2_w = [tile("z2_w%d" % c, [P, CHUNKS[c]], U32) for c in chunks]
+        z2_sc = [tile("z2_sc%d" % c, [P, CHUNKS[c]], U8) for c in chunks]
+        o = [tile("o%d" % c, [P, PACK, CHUNKS[c]], F32) for c in chunks]
+        o_bf = tile("o_bf", [P, PACK * U], BF16)
+        o_w = tile("o_w", [P, U], I32)
 
         def project(c):
-            cols = slice(c * CHUNK, (c + 1) * CHUNK)
-            nc.vector.quantize_mx(out=z2_w[c][:].bitcast(FP8X4), scales=z2_sc[c][:], in_=z2_bf[c][:].rearrange("p w t -> p (w t)"))
+            nc.vector.quantize_mx(out=z2_w[c][:].bitcast(FP8X4), scales=z2_sc[c][:], in_=z2_bf[:, PACK * cols_of[c].start : PACK * cols_of[c].stop])
+            per_bank = S // CHUNKS[c]
             accs = []
-            for pair in range(2):
-                acc = bank(2 * c + pair, [P, 2, CHUNK])
+            for b in range(PACK // per_bank):
+                acc = bank(cols_of[c].start // P + b, [P, per_bank, CHUNKS[c]])
                 accs.append(acc)
-                for e in range(2):
-                    t = 2 * pair + e
+                for e in range(per_bank):
+                    t = per_bank * b + e
                     nc.tensor.matmul_mx(
                         out=acc[:, e, :], lhsT=w2_wd[:, 256 * t : 256 * (t + 1)].bitcast(FP4X4), lhsT_scale=w2_sd[:, P * t : P * (t + 1)],
                         rhs=z2_w[c][:].bitcast(FP8X4), rhs_scale=z2_sc[c][:], start=True, stop=True,
@@ -212,26 +251,29 @@ def tile_picked_pqktrackpaget_none_po_kernel(
             return accs
 
         def add_residual(c, accs):
-            cols = slice(c * CHUNK, (c + 1) * CHUNK)
-            for pair in range(2):
-                ts = slice(2 * pair, 2 * pair + 2)
-                nc.vector.tensor_tensor(o[c][:, ts, :], accs[pair][:], res_t[:, ts, cols], ALU.add)
-            nc.sync.dma_start(out=out_rows[:, :, cols], in_=o[c][:])
-            nc.scalar.copy(woven(o_bf[c][:]), by_rows(o[c][:]))
+            per_bank = S // CHUNKS[c]
+            for b, acc in enumerate(accs):
+                ts = slice(per_bank * b, per_bank * (b + 1))
+                nc.vector.tensor_tensor(o[c][:, ts, :], acc[:], res_t[:, ts, cols_of[c]], ALU.add)
+            nc.sync.dma_start(out=out_rows[:, :, cols_of[c]], in_=o[c][:])
+            if c < len(CHUNKS) - 1:
+                nc.scalar.copy(woven(o_bf[:, words_of(cols_of[c])]), by_rows(o[c][:]))
+            else:
+                nc.vector.tensor_copy(woven(o_bf[:, words_of(cols_of[c])]), by_rows(o[c][:]))
 
-        def hand_on(c):
-            cols = slice(c * CHUNK, (c + 1) * CHUNK)
-            nc.vector.quantize_mx(out=o_w[c][:].bitcast(FP8X4), scales=o_sc[:, cols], in_=o_bf[c][:])
-            nc.sync.dma_start(out=out_words[:, cols], in_=o_w[c][:])
+        def hand_on(cols):
+            nc.vector.quantize_mx(out=o_w[:, cols].bitcast(FP8X4), scales=o_sc[:, cols], in_=o_bf[:, words_of(cols)])
+            nc.sync.dma_start(out=out_words[:, cols], in_=o_w[:, cols])
 
-        accs = {}
-        n = len(chunks)
-        for step in range(n + 2):
-            if step < n:
-                accs[step] = project(step)
-            if 1 <= step <= n:
-                add_residual(step - 1, accs[step - 1])
-            if step >= 2:
-                hand_on(step - 2)
+        accs = [project(0)]
+        round_on_vector(slice(CHUNKS[0], ON_VECTOR))
+        accs.extend(project(c) for c in chunks[1:])
+        for c in chunks[:-1]:
+            add_residual(c, accs[c])
+        hand_on(slice(0, 512))
+        add_residual(chunks[-1], accs[-1])
+        hand_on(slice(512, 768))
+        hand_on(slice(768, U))
         for q in range(4):
-            nc.sync.dma_start(out=out_2[0, 4 * q : 4 * q + 4, :].bitcast(I32), in_=o_sc[32 * q : 32 * q + 4, :].bitcast(I32))
+            eng = nc.sync if q % 2 == 0 else nc.scalar
+            eng.dma_start(out=out_2[0, 4 * q : 4 * q + 4, :].bitcast(I32), in_=o_sc[32 * q : 32 * q + 4, :].bitcast(I32))

from contextlib import ExitStack

import concourse.mybir as mybir

FLOPS = 1073741824

F32 = mybir.dt.float32
BF16 = mybir.dt.bfloat16
I32 = mybir.dt.int32
U32 = mybir.dt.uint32
U16 = mybir.dt.uint16
U8 = mybir.dt.uint8
FP8X4 = mybir.dt.float8_e4m3fn_x4
FP4X4 = mybir.dt.float4_e2m1fn_x4
ACT = mybir.ActivationFunctionType
ALU = mybir.AluOpType

P = 128
PACK = 4
S = 512
T = 1024
G = 2048
U = 1024
HALF = 256
CHUNKS = (128, 256, 256, 256, 128)
SCALED_ON_SCALAR = 1
ON_VECTOR = 256


def load_scale_rows(queue, plane, scales):
    for q in range(4):
        queue.dma_start(out=plane[32 * q : 32 * q + 4, :].bitcast(I32), in_=scales[0, 4 * q : 4 * q + 4, :].bitcast(I32))


def deal(engine, out, in_, width):
    engine.tensor_copy(
        out=out.rearrange("p (t m b) -> p t m b", t=PACK, b=width),
        in_=in_.rearrange("p (m t b) -> p t m b", t=PACK, b=width),
    )


def words_of(cols):
    return slice(PACK * cols.start, PACK * cols.stop)


def woven(ap):
    return ap.rearrange("p (c i t) -> p c t i", i=4, t=PACK)


def by_rows(ap):
    return ap.rearrange("p t (c i) -> p c t i", i=4)


def tile_picked_pqktrackpaget_none_po_kernel(
    tc, x_words, x_scales, w1_words, w1_scales, gs, d_words, d_scales, mem, res, gn, w2_words, w2_scales,
    offs, n1, n2, kidx, n3, out_0, out_1, out_2,
):
    nc = tc.nc
    with ExitStack() as ctx:
        sb = ctx.enter_context(tc.tile_pool(name="sb", bufs=1))
        ps = ctx.enter_context(tc.psum_pool(name="ps", bufs=1))

        def tile(name, shape, dtype):
            return sb.tile(shape, dtype, name=name, align_bytes=64)

        def bank(n, shape):
            return ps.tile(shape, F32, name="bank%d" % n, tag="bank%d" % n)

        def load_list(name, src):
            t = sb.tile([P, S // 16], U16, name=name)
            nc.sync.dma_start(t[:], src)
            return t

        x_sc = tile("x_sc", [P, T], U8)
        w1_sc = tile("w1_sc", [P, S], U8)
        w2_sc = tile("w2_sc", [P, S], U8)
        d_sc = tile("d_sc", [P, G], U8)
        key_sc = tile("key_sc", [P, S], U8)
        nc.vector.memset(x_sc[:].bitcast(I32), 0)
        nc.gpsimd.memset(w1_sc[:].bitcast(I32), 0)
        nc.vector.memset(d_sc[:].bitcast(I32), 0)
        nc.gpsimd.memset(w2_sc[:].bitcast(I32), 0)
        nc.gpsimd.memset(key_sc[:].bitcast(I32), 0)
        warm = tile("warm", [P, 2], F32)
        nc.gpsimd.memset(warm[:, 0:1], 0.0)
        nc.scalar.activation(warm[:, 1:2], warm[:, 0:1], ACT.Sigmoid)

        w1_w = tile("w1_w", [P, 2 * S], U8)
        nc.sync.dma_start(out=w1_w[:].bitcast(I32), in_=w1_words[0].bitcast(I32))
        load_scale_rows(nc.sync, x_sc, x_scales)
        offs_t = load_list("offs_t", offs)
        x_w = tile("x_w", [P, T], I32)
        nc.sync.dma_start(out=x_w[:], in_=x_words[0].rearrange("p c r -> p (c r)").bitcast(I32))
        kidx_t = load_list("kidx_t", kidx)
        load_scale_rows(nc.sync, w1_sc, w1_scales)
        d_w = tile("d_w", [P, G], I32)
        nc.sync.dma_start(out=d_w[:], in_=d_words[0].rearrange("p c r -> p (c r)").bitcast(I32))
        nc.sync.dma_start(out=d_sc[0:P:8, :].bitcast(I32), in_=d_scales[0].bitcast(I32))
        n1_t = load_list("n1_t", n1)
        n2_t = load_list("n2_t", n2)
        gs_t = tile("gs_t", [P, PACK], F32)
        nc.gpsimd.dma_start(out=gs_t[:], in_=gs.rearrange("(p t) o -> p (t o)", t=PACK))

        w2_w = tile("w2_w", [P, 2 * S], U8)
        nc.gpsimd.dma_start(out=w2_w[:].bitcast(I32), in_=w2_words[0].bitcast(I32))
        load_scale_rows(nc.gpsimd, w2_sc, w2_scales)
        w2_wd = tile("w2_wd", [P, 2 * S], U8)
        w2_sd = tile("w2_sd", [P, S], U8)
        deal(nc.gpsimd, w2_wd[:], w2_w[:], 2)
        deal(nc.gpsimd, w2_sd[:], w2_sc[:], 1)

        w1_wd = tile("w1_wd", [P, 2 * S], U8)
        w1_sd = tile("w1_sd", [P, S], U8)
        xg_sc = tile("xg_sc", [P, S], U8)
        xg_w = tile("xg_w", [P, S], U32)
        deal(nc.vector, w1_wd[:], w1_w[:], 2)
        nc.vector.tensor_copy(xg_sc[:], x_sc[:].indirect(offs_t[:]))
        nc.vector.tensor_copy(xg_w[:], x_w[:].bitcast(U32).indirect(offs_t[:]))
        deal(nc.vector, w1_sd[:], w1_sc[:], 1)
        y_ps = [bank(t, [P, S]) for t in range(PACK)]
        for t in range(PACK):
            nc.tensor.matmul_mx(
                out=y_ps[t][:], lhsT=w1_wd[:, 256 * t : 256 * (t + 1)].bitcast(FP4X4), lhsT_scale=w1_sd[:, P * t : P * (t + 1)],
                rhs=xg_w[:].bitcast(FP8X4), rhs_scale=xg_sc[:], start=True, stop=True,
            )

        dg_sc = tile("dg_sc", [P, S], U8)
        dg_sd = sb.tile([P, S], U8, name="dg_sd", tag="late", align_bytes=64)
        dg_w = tile("dg_w", [P, S], U32)
        key_w = tile("key_w", [P, S], U32)
        nc.vector.tensor_copy(dg_w[:], d_w[:].bitcast(U32).indirect(kidx_t[:]))
        nc.vector.tensor_copy(dg_sc[:], d_sc[:].indirect(kidx_t[:]))
        deal(nc.vector, key_w[:], dg_w[:], 1)
        deal(nc.vector, dg_sd[:], dg_sc[:], 1)

        n3_t = load_list("n3_t", n3)
        mem_rows = mem.rearrange("(p t) w -> p t w", t=PACK)
        page = [sb.tile([P, U], F32, name="page%d" % t) for t in range(PACK)]
        for t in range(PACK):
            nc.sync.dma_start(out=page[t][:], in_=mem_rows[:, t, :])
        for j in range(4):
            nc.sync.dma_start(out=key_sc[j:P:32, :].bitcast(I32), in_=dg_sd[8 * j : P : 32, :].bitcast(I32))
        gn_t = tile("gn_t", [P, PACK], F32)
        nc.sync.dma_start(out=gn_t[:], in_=gn.rearrange("(p t) o -> p (t o)", t=PACK))
        res_t = sb.tile([P, PACK, U], F32, name="res_t", tag="late", align_bytes=64)
        nc.sync.dma_start(out=res_t[:], in_=res.rearrange("(p t) w -> p t w", t=PACK))

        halves = range(S // HALF)
        y = [tile("y%d" % t, [P, S], F32) for t in range(PACK)]
        ys = [tile("ys%d" % t, [P, S], F32) for t in range(PACK)]
        gate = [tile("gate%d" % h, [P, PACK, HALF], F32) for h in halves]
        far = [tile("far%d" % h, [P, PACK, HALF], F32) for h in halves]
        near = [tile("near%d" % h, [P, PACK, HALF], F32) for h in halves]
        z_bf = [tile("z_bf%d" % h, [P, PACK * HALF], BF16) for h in halves]
        z_w = [tile("z_w%d" % h, [P, HALF], U32) for h in halves]
        z_sc = [tile("z_sc%d" % h, [P, HALF], U8) for h in halves]
        s_ps = [bank(4 + t, [P, S]) for t in range(PACK)]
        keep = [tile("keep%d" % t, [P, S], F32) for t in range(PACK)]
        kept = [tile("kept%d" % t, [P, S], F32) for t in range(PACK)]
        fresh = [tile("fresh%d" % t, [P, S], F32) for t in range(PACK)]
        lcols = HALF // 16

        def half(h):
            return slice(h * HALF, (h + 1) * HALF)

        def list_half(lst, h):
            return lst[:, h * lcols : (h + 1) * lcols]

        def blend_terms(h, t):
            nc.scalar.activation(gate[h][:, t, :], y[t][:].indirect(list_half(n1_t, h)), ACT.Sigmoid)
            nc.vector.scalar_tensor_tensor(near[h][:, t, :], gate[h][:, t, :], 1.0, ys[t][:, half(h)], ALU.subtract, ALU.mult)
            nc.vector.tensor_tensor(far[h][:, t, :], ys[t][:].indirect(list_half(n2_t, h)), gate[h][:, t, :], ALU.mult)

        def blend(h):
            nc.vector.tensor_tensor(woven(z_bf[h][:]), by_rows(far[h][:]), by_rows(near[h][:]), ALU.subtract)

        def score(h):
            nc.vector.quantize_mx(out=z_w[h][:].bitcast(FP8X4), scales=z_sc[h][:], in_=z_bf[h][:])
            for t in range(PACK):
                nc.tensor.matmul_mx(
                    out=s_ps[t][:, half(h)], lhsT=key_w[:, P * t : P * (t + 1)].bitcast(FP8X4), lhsT_scale=key_sc[:, P * t : P * (t + 1)],
                    rhs=z_w[h][:].bitcast(FP8X4), rhs_scale=z_sc[h][:], start=True, stop=True,
                )
                nc.scalar.activation(keep[t][:, half(h)], s_ps[t][:, half(h)], ACT.Sigmoid, scale=-0.0625)

        def weigh_old_half(h, t):
            nc.vector.tensor_tensor(kept[t][:, half(h)], page[t][:].indirect(list_half(n3_t, h)), keep[t][:, half(h)], ALU.mult)

        for t in range(PACK):
            nc.scalar.copy(y[t][:], y_ps[t][:])
            if t < SCALED_ON_SCALAR:
                nc.scalar.activation(ys[t][:], y_ps[t][:], ACT.Copy, scale=gs_t[:, t : t + 1])
            else:
                nc.vector.tensor_scalar(ys[t][:], y[t][:], gs_t[:, t : t + 1], None, ALU.mult)
            blend_terms(0, t)
        blend_terms(1, 0)
        blend(0)
        blend_terms(1, 1)
        score(0)
        blend_terms(1, 2)
        blend_terms(1, 3)
        weigh_old_half(0, 0)
        blend(1)
        weigh_old_half(0, 1)
        score(1)
        weigh_old_half(0, 2)
        weigh_old_half(0, 3)
        for t in range(PACK):
            weigh_old_half(1, t)
        for t in range(PACK):
            nc.scalar.activation(fresh[t][:], s_ps[t][:], ACT.Silu, scale=0.0625)

        chunks = range(len(CHUNKS))
        cols_of = [slice(sum(CHUNKS[:c]), sum(CHUNKS[: c + 1])) for c in chunks]
        z2_bf = tile("z2_bf", [P, U * PACK], BF16)
        z2_rows = z2_bf[:].rearrange("p (w t) -> p w t", t=PACK)
        for t in range(PACK):
            nc.vector.tensor_tensor(page[t][:].indirect(n3_t[:]), kept[t][:], fresh[t][:], ALU.add)
            spans = [[slice(0, U)], [slice(0, U)], [slice(ON_VECTOR, U)], [slice(max(cols.start, ON_VECTOR), cols.stop) for cols in cols_of[1:]]][t]
            for cols in spans:
                nc.scalar.activation(z2_rows[:, cols, t], page[t][:, cols], ACT.Copy, scale=gn_t[:, t : t + 1])

        def round_on_vector(cols):
            for t in (2, 3):
                nc.vector.tensor_scalar(z2_rows[:, cols, t], page[t][:, cols], gn_t[:, t : t + 1], None, ALU.mult)

        round_on_vector(cols_of[0])

        out_rows = out_0.rearrange("(p t) w -> p t w", t=PACK)
        out_words = out_1[0].rearrange("p c r -> p (c r)").bitcast(I32)
        o_sc = tile("o_sc", [P, U], U8)
        z2_w = [tile("z2_w%d" % c, [P, CHUNKS[c]], U32) for c in chunks]
        z2_sc = [tile("z2_sc%d" % c, [P, CHUNKS[c]], U8) for c in chunks]
        o = [tile("o%d" % c, [P, PACK, CHUNKS[c]], F32) for c in chunks]
        o_bf = tile("o_bf", [P, PACK * U], BF16)
        o_w = tile("o_w", [P, U], I32)

        def project(c):
            nc.vector.quantize_mx(out=z2_w[c][:].bitcast(FP8X4), scales=z2_sc[c][:], in_=z2_bf[:, PACK * cols_of[c].start : PACK * cols_of[c].stop])
            per_bank = S // CHUNKS[c]
            accs = []
            for b in range(PACK // per_bank):
                acc = bank(cols_of[c].start // P + b, [P, per_bank, CHUNKS[c]])
                accs.append(acc)
                for e in range(per_bank):
                    t = per_bank * b + e
                    nc.tensor.matmul_mx(
                        out=acc[:, e, :], lhsT=w2_wd[:, 256 * t : 256 * (t + 1)].bitcast(FP4X4), lhsT_scale=w2_sd[:, P * t : P * (t + 1)],
                        rhs=z2_w[c][:].bitcast(FP8X4), rhs_scale=z2_sc[c][:], start=True, stop=True,
                    )
            return accs

        def add_residual(c, accs):
            per_bank = S // CHUNKS[c]
            for b, acc in enumerate(accs):
                ts = slice(per_bank * b, per_bank * (b + 1))
                nc.vector.tensor_tensor(o[c][:, ts, :], acc[:], res_t[:, ts, cols_of[c]], ALU.add)
            nc.sync.dma_start(out=out_rows[:, :, cols_of[c]], in_=o[c][:])
            if c < len(CHUNKS) - 1:
                nc.scalar.copy(woven(o_bf[:, words_of(cols_of[c])]), by_rows(o[c][:]))
            else:
                nc.vector.tensor_copy(woven(o_bf[:, words_of(cols_of[c])]), by_rows(o[c][:]))

        def hand_on(cols):
            nc.vector.quantize_mx(out=o_w[:, cols].bitcast(FP8X4), scales=o_sc[:, cols], in_=o_bf[:, words_of(cols)])
            nc.sync.dma_start(out=out_words[:, cols], in_=o_w[:, cols])

        accs = [project(0)]
        round_on_vector(slice(CHUNKS[0], ON_VECTOR))
        accs.extend(project(c) for c in chunks[1:])
        for c in chunks[:-1]:
            add_residual(c, accs[c])
        hand_on(slice(0, 512))
        add_residual(chunks[-1], accs[-1])
        hand_on(slice(512, 768))
        hand_on(slice(768, U))
        for q in range(4):
            eng = nc.sync if q % 2 == 0 else nc.scalar
            eng.dma_start(out=out_2[0, 4 * q : 4 * q + 4, :].bitcast(I32), in_=o_sc[32 * q : 32 * q + 4, :].bitcast(I32))
